import numpy as np
import ml_dtypes


def mxq(x, axis, fmt="e4m3"):
    dtype, down = {"e4m3": (ml_dtypes.float8_e4m3fn, 7), "e5m2": (ml_dtypes.float8_e5m2, 14)}[fmt]
    v = np.moveaxis(np.asarray(x, np.float32).astype(ml_dtypes.bfloat16).astype(np.float64), axis, -1)
    blocks = v.reshape(v.shape[:-1] + (-1, 32))
    amax = np.abs(blocks).max(-1, keepdims=True)
    byte = np.maximum(np.where(amax > 0, np.frexp(amax)[1] - 1 + 127, 0) - down, 1)
    scale = np.exp2(byte - 127.0)
    codes = (blocks / scale).astype(np.float32).astype(dtype).astype(np.float64)
    return np.moveaxis((codes * scale).reshape(v.shape), -1, axis)


WIDE = False


def mx_kscale(k):
    if not WIDE:
        return np.ones(k)
    levels = np.array([10, -10, 5, -5, 0])
    if k % 512:
        return np.exp2(np.random.permutation(np.resize(levels, k // 32))).repeat(32)
    a = np.empty((k // 512, 16))
    for p in range(k // 512):
        a[p, :8] = np.random.permutation(np.resize(levels, 8))
        for g in range(8):
            far = levels[np.abs(levels - a[p, g]) >= 10]
            a[p, g + 8] = far[np.random.randint(len(far))]
    return np.exp2(a.ravel()).repeat(32)


BF16 = ml_dtypes.bfloat16


def bf(x):
    return np.asarray(x, np.float32).astype(BF16)


def f64(x):
    return np.asarray(x).astype(np.float64)


E2M1 = np.array([0.0, 0.5, 1.0, 1.5, 2.0, 3.0, 4.0, 6.0, -0.0, -0.5, -1.0, -1.5, -2.0, -3.0, -4.0, -6.0])


def pack_weight(w, fmt):
    k, n = w.shape
    w = f64(bf(w)).reshape(k // 32, 32, n)
    amax = np.abs(w).max(1)
    if fmt == "e4m3":
        byte = np.frexp(amax)[1] - 1 + 127 - 7
    else:
        mant, ex = np.frexp(amax / 6.0)
        byte = np.where(mant > 0.5, ex, ex - 1) + 127
    byte = np.clip(np.where(amax > 0, byte, 1), 1, 254)
    scaled = (w * np.exp2(127.0 - byte)[:, None, :]).reshape(k, n).astype(np.float32)
    by_word = np.ascontiguousarray(scaled.reshape(k // 512, 128, 4, n).transpose(0, 1, 3, 2))
    if fmt == "e4m3":
        words = by_word.astype(ml_dtypes.float8_e4m3fn).view(np.uint8)
    else:
        c = by_word.astype(ml_dtypes.float4_e2m1fn).view(np.uint8) & 0xF
        words = c[..., 0::2] | (c[..., 1::2] << 4)
    return np.ascontiguousarray(words), np.ascontiguousarray(byte.astype(np.uint8).reshape(k // 512, 16, n))


def unpack_weight(words, scales, fmt):
    g, p, n, _ = words.shape
    if fmt == "e4m3":
        vals = np.ascontiguousarray(words).view(ml_dtypes.float8_e4m3fn).astype(np.float64)
    else:
        nib = np.empty((g, p, n, 4), np.uint8)
        nib[..., 0::2] = words & 0xF
        nib[..., 1::2] = words >> 4
        vals = E2M1[nib]
    vals = vals * np.repeat(np.exp2(scales.astype(np.float64) - 127.0), 8, axis=1)[..., None]
    return vals.transpose(0, 1, 3, 2).reshape(g * 512, n)
def pack4(w):
    words, scales = pack_weight(w, "e2m1")
    return words.reshape(words.shape[0], 128, -1), scales


def unpack4(words, scales):
    return unpack_weight(words.reshape(words.shape[0], 128, -1, 2), scales, "e2m1")


def planes(Y):
    n, m = Y.shape
    b = f64(bf(Y)).reshape(n // 32, 32, m)
    amax = np.abs(b).max(1)
    byte = np.clip(np.where(amax > 0, np.frexp(amax)[1] - 1 + 127 - 7, 1), 1, 254)
    codes = (b * np.exp2(127.0 - byte)[:, None, :]).reshape(n, m).astype(np.float32).astype(ml_dtypes.float8_e4m3fn).view(np.uint8)
    words = codes.reshape(n // 512, 128, 4, m).transpose(0, 1, 3, 2)
    return np.ascontiguousarray(words), np.ascontiguousarray(byte.astype(np.uint8).reshape(n // 512, 16, m))


T, K = 1536, 1024
STAY, PEAK = 0.8, 0.75

def setup_inputs():
    a = (0.4 + 0.6 * np.random.rand(T, 1)) * 2.0 * np.random.rand(T, K)
    P = np.exp(2.0 * np.random.randn(K, K))
    P = STAY * P / P.sum(axis=1, keepdims=True)
    R = np.linalg.inv(np.eye(K) - P)
    lam = np.linalg.solve(np.eye(K) - P.T, a.T)
    mu = lam.max(axis=1) / PEAK
    g = np.exp(0.7 * np.random.randn(K))
    C = g * (1.5 / K + np.random.randn(K, K) / np.sqrt(K))
    E = 0.7 * g * np.random.randn(K, K) / np.sqrt(K)
    s = mx_kscale(K)[:, None]
    x_words, x_scales = pack_weight(a.T * s, "e4m3")
    c_words, c_scales = pack4(C / s)
    e_words, e_scales = pack_weight(E / s, "e4m3")
    return {"x_words": x_words, "x_scales": x_scales, "v": bf(R / mu / s),
            "c_words": c_words, "c_scales": c_scales, "e_words": e_words, "e_scales": e_scales}

def reference(x_words, x_scales, v, c_words, c_scales, e_words, e_scales):
    x = unpack_weight(x_words, x_scales, "e4m3")
    c = unpack4(c_words, c_scales)
    e = unpack_weight(e_words, e_scales, "e4m3")
    rho = x.T @ mxq(f64(v), 0, "e4m3")
    price = x.T @ c
    charge = x.T @ e
    y = price * (rho / (1.0 - rho)) + charge
    Y = y.T
    words, scales = planes(Y)
    return y, words, scales

@@ -1,0 +1,306 @@
+from contextlib import ExitStack
+
+import concourse.mybir as mybir
+from concourse.masks import make_identity
+
+T, K = 1536, 1024
+FLOPS = 3 * 2 * T * K * K
+
+F32 = mybir.dt.float32
+BF16 = mybir.dt.bfloat16
+I32 = mybir.dt.int32
+U32 = mybir.dt.uint32
+U8 = mybir.dt.uint8
+FP8X4 = mybir.dt.float8_e4m3fn_x4
+FP4X4 = mybir.dt.float4_e2m1fn_x4
+ALU = mybir.AluOpType
+ACT = mybir.ActivationFunctionType
+
+P = 128
+PASSES = 2
+HALF = 512
+TILES = T // P
+UNITS = 2 * TILES
+X_CHUNKS = ((0, 384), (384, 896), (896, 1536))
+RING = 4
+YB_RING = 8
+
+
+def tile_jackson_congestion_cost_k3_kernel(
+    tc, x_words, x_scales, v, c_words, c_scales, e_words, e_scales, out_0, out_1, out_2
+):
+    nc = tc.nc
+    with ExitStack() as ctx:
+        keep = ctx.enter_context(tc.tile_pool(name="keep", bufs=1))
+        psum = ctx.enter_context(tc.psum_pool(name="psum", bufs=1))
+        ctx.enter_context(tc.manual_schedule())
+
+        def sb(name, shape, dtype):
+            return keep.tile(shape, dtype, name=name, align_bytes=64)
+
+        banks = [psum.tile([P, HALF], F32, name="bank%d" % b) for b in range(8)]
+        rho_banks, price_banks, charge_banks, turn_banks = banks[0:2], banks[2:4], banks[4:6], banks[6:8]
+
+        xw = [sb("xw%d" % j, [P, PASSES, b - a], U32) for j, (a, b) in enumerate(X_CHUNKS)]
+        xs = sb("xs", [P, PASSES, T], U8)
+        cw = [sb("cw%d" % h, [P, PASSES, 2 * HALF], U8) for h in range(2)]
+        cs = sb("cs", [P, PASSES, K], U8)
+        ew = [sb("ew%d" % h, [P, PASSES, HALF], U32) for h in range(2)]
+        es = sb("es", [P, PASSES, K], U8)
+        v_raw = [[sb("vraw%d%d" % (h, g), [P, 4, HALF], BF16) for g in range(PASSES)] for h in range(2)]
+        v_grp = [[sb("vgrp%d%d" % (h, g), [P, HALF, 4], BF16) for g in range(PASSES)] for h in range(2)]
+        vw = [[sb("vw%d%d" % (h, g), [P, HALF], U32) for g in range(PASSES)] for h in range(2)]
+        vs = [[sb("vs%d%d" % (h, g), [P, HALF], U8) for g in range(PASSES)] for h in range(2)]
+        one = sb("one", [P, 1], F32)
+        warm = sb("warm", [P, 1], F32)
+        ident = sb("ident", [P, P], F32)
+        sq_t = [sb("sq%d" % j, [P, HALF], F32) for j in range(RING)]
+        inv_t = [sb("inv%d" % j, [P, HALF], F32) for j in range(RING)]
+        jobs_t = [sb("jobs%d" % j, [P, HALF], F32) for j in range(RING)]
+        cost_t = [sb("cost%d" % j, [P, HALF], F32) for j in range(RING)]
+        y_t = [sb("y%d" % j, [P, HALF], F32) for j in range(UNITS)]
+        yb_t = [sb("yb%d" % j, [P, HALF], BF16) for j in range(YB_RING)]
+        y_grp = [sb("ygrp%d" % j, [P, 2 * HALF], BF16) for j in range(RING)]
+        yw = [sb("yw%d" % h, [P, T], U32) for h in range(2)]
+        ys = [sb("ys%d" % h, [P, T], U8) for h in range(2)]
+
+        def load_v(h, g):
+            rows = v[g * 512 : (g + 1) * 512, h * HALF : (h + 1) * HALF]
+            nc.sync.dma_start(out=v_raw[h][g][:], in_=rows.rearrange("(p t) n -> p t n", t=4))
+
+        def load_scales(plane, src):
+            rows = src.rearrange("g (q r) n -> r q g n", r=4)
+            for r in range(4):
+                nc.sync.dma_start(out=plane[r:P:32, :, :].bitcast(I32), in_=rows[r].bitcast(I32))
+
+        def load_x(j):
+            a, b = X_CHUNKS[j]
+            src = x_words.rearrange("g p n t -> p g (n t)")[:, :, 4 * a : 4 * b]
+            nc.sync.dma_start(out=xw[j][:].bitcast(I32), in_=src.bitcast(I32))
+
+        def load_c(h):
+            src = c_words.rearrange("g p b -> p g b")[:, :, 2 * HALF * h : 2 * HALF * (h + 1)]
+            nc.sync.dma_start(out=cw[h][:].bitcast(I32), in_=src.bitcast(I32))
+
+        def load_e(h):
+            src = e_words.rearrange("g p n t -> p g (n t)")[:, :, 4 * HALF * h : 4 * HALF * (h + 1)]
+            nc.sync.dma_start(out=ew[h][:].bitcast(I32), in_=src.bitcast(I32))
+
+        def interleave_v(engine, h, g, a, b):
+            dst = v_grp[h][g][:, a:b, :]
+            src = v_raw[h][g][:, :, a:b]
+            if engine == "gpsimd":
+                nc.gpsimd.tensor_scalar(dst, src.rearrange("p t n -> p n t"), 1.0, 1.0, ALU.mult, ALU.mult)
+                return
+            dst = dst.rearrange("p (c i) t -> p c t i", i=4)
+            src = src.rearrange("p t (c i) -> p c t i", i=4)
+            if engine == "vector":
+                nc.vector.tensor_copy(out=dst, in_=src)
+            else:
+                nc.scalar.copy(out=dst, in_=src)
+
+        def quantize_v(h, g):
+            nc.vector.quantize_mx(
+                out=vw[h][g][:].bitcast(FP8X4),
+                scales=vs[h][g][:],
+                in_=v_grp[h][g][:].rearrange("p n t -> p (n t)"),
+            )
+
+        def mx_pass(bank, u, g, rhs, rhs_scale):
+            m0 = (u % TILES) * P
+            j = [a <= m0 < b for a, b in X_CHUNKS].index(True)
+            off = m0 - X_CHUNKS[j][0]
+            nc.tensor.matmul_mx(
+                out=bank[:],
+                lhsT=xw[j][:, g, off : off + P].bitcast(FP8X4),
+                lhsT_scale=xs[:, g, m0 : m0 + P],
+                rhs=rhs,
+                rhs_scale=rhs_scale,
+                start=(g == 0),
+                stop=(g == PASSES - 1),
+            )
+
+        def rho_bank(u):
+            if u < 2:
+                return rho_banks[u]
+            if u == 2:
+                return turn_banks[0]
+            return rho_banks[(u + 1) % 2]
+
+        def rho_pass(u, g):
+            h = u // TILES
+            mx_pass(rho_bank(u), u, g, vw[h][g][:].bitcast(FP8X4), vs[h][g][:])
+
+        def rho(u):
+            for g in range(PASSES):
+                rho_pass(u, g)
+
+        def price(u):
+            h = u // TILES
+            for g in range(PASSES):
+                mx_pass(price_banks[u % 2], u, g, cw[h][:, g, :].bitcast(FP4X4), cs[:, g, h * HALF : (h + 1) * HALF])
+
+        def charge(u):
+            h = u // TILES
+            for g in range(PASSES):
+                mx_pass(charge_banks[u % 2], u, g, ew[h][:, g, :].bitcast(FP8X4), es[:, g, h * HALF : (h + 1) * HALF])
+
+        def square(u):
+            nc.scalar.activation(sq_t[u % RING][:], rho_bank(u)[:], ACT.Square, bias=one[:], scale=-1.0)
+
+        def invert(u):
+            nc.scalar.activation(inv_t[u % RING][:], sq_t[u % RING][:], ACT.Abs_reciprocal_sqrt)
+
+        def jobs(u):
+            nc.vector.tensor_tensor(jobs_t[u % RING][:], rho_bank(u)[:], inv_t[u % RING][:], ALU.mult)
+
+        def cost(u):
+            nc.vector.tensor_tensor(cost_t[u % RING][:], price_banks[u % 2][:], jobs_t[u % RING][:], ALU.mult)
+
+        def total(u):
+            nc.vector.tensor_tensor(y_t[u][:], charge_banks[u % 2][:], cost_t[u % RING][:], ALU.add)
+
+        def pairs_in(ap):
+            return ap.rearrange("p (m w e) -> p w m e", w=2, e=2)
+
+        def pairs_out(u):
+            return yb_t[u % YB_RING][:].rearrange("p (w m e) -> p w m e", w=2, e=2)
+
+        def cast(u):
+            nc.gpsimd.tensor_scalar(pairs_out(u), pairs_in(y_t[u][:]), 1.0, 1.0, ALU.mult, ALU.mult)
+
+        def total_bf16(u):
+            nc.vector.tensor_tensor(
+                pairs_out(u), pairs_in(charge_banks[u % 2][:]), pairs_in(cost_t[u % RING][:]), ALU.add
+            )
+
+        def store_y(u):
+            h, i = divmod(u, TILES)
+            nc.sync.dma_start(out=out_0[i * P : (i + 1) * P, h * HALF : (h + 1) * HALF], in_=y_t[u][:])
+
+        def turn(bank, u0, n):
+            for i in range(n):
+                words = yb_t[(u0 + i) % YB_RING][:].bitcast(F32)
+                for w in range(2):
+                    c0 = (2 * i + w) * P
+                    nc.tensor.transpose(bank[:, c0 : c0 + P], words[:, w * P : (w + 1) * P], ident[:])
+
+        def gather(slot, bank, n):
+            dst = y_grp[slot][:, 0 : n * HALF].bitcast(F32).rearrange("p (i m w) -> p i m w", i=n, w=2)
+            src = bank[:, 0 : n * 2 * P].rearrange("p (i w m) -> p i m w", i=n, w=2)
+            nc.scalar.copy(out=dst, in_=src)
+
+        def quantize_y(slot, u0, n):
+            h, i = divmod(u0, TILES)
+            cols = slice(i * P, (i + n) * P)
+            nc.vector.quantize_mx(
+                out=yw[h][:, cols].bitcast(FP8X4), scales=ys[h][:, cols], in_=y_grp[slot][:, 0 : n * HALF]
+            )
+
+        def store_words(u0, n):
+            h, i = divmod(u0, TILES)
+            dst = out_1[h].rearrange("p m t -> p (m t)")[:, 4 * i * P : 4 * (i + n) * P]
+            nc.sync.dma_start(out=dst.bitcast(I32), in_=yw[h][:, i * P : (i + n) * P].bitcast(I32))
+
+        def store_scales(h, queues):
+            for q in range(4):
+                queues[q].dma_start(
+                    out=out_2[h, 4 * q : 4 * q + 4, :].bitcast(I32), in_=ys[h][32 * q : 32 * q + 4, :].bitcast(I32)
+                )
+
+        load_v(0, 0)
+        load_v(0, 1)
+        nc.gpsimd.memset(one[:], 1.0)
+        nc.scalar.activation(warm[:], one[:], ACT.Abs_reciprocal_sqrt)
+        for plane in (xs, cs, es):
+            nc.vector.memset(plane[:].bitcast(I32), 0)
+        make_identity(nc, ident[:])
+        load_scales(xs, x_scales)
+        load_x(0)
+        load_scales(cs, c_scales)
+        load_c(0)
+        load_scales(es, e_scales)
+        load_e(0)
+        load_x(1)
+        load_v(1, 0)
+        load_v(1, 1)
+        load_x(2)
+        load_c(1)
+        load_e(1)
+
+        interleave_v("vector", 0, 0, 0, 320)
+        interleave_v("scalar", 0, 0, 320, 512)
+        quantize_v(0, 0)
+        interleave_v("scalar", 0, 1, 256, 512)
+        interleave_v("vector", 0, 1, 0, 256)
+        quantize_v(0, 1)
+        rho_pass(0, 0)
+        rho_pass(1, 0)
+        rho_pass(0, 1)
+        rho_pass(1, 1)
+        square(0)
+        invert(0)
+        square(1)
+        invert(1)
+        jobs(0)
+
+        scalar_v = {2: (0, 256), 3: (0, 384), 4: (1, 128), 7: (1, 256), 8: (1, 384)}
+        gpsimd_v = {1: (0, 0), 2: (0, 128), 3: (1, 0)}
+        quant_v = {5: 0, 9: 1}
+        last = UNITS - 1
+        for k in range(UNITS):
+            b, phase = divmod(k - 5, 4)
+            price(k)
+            if k == 0:
+                charge(0)
+            if k >= 5 and phase == 0:
+                turn(turn_banks[0], 4 * b, 2)
+                turn(turn_banks[1], 4 * b + 2, 2)
+            if k + 2 <= last:
+                rho(k + 2)
+            if k > 0:
+                charge(k)
+            cost(k)
+            if k + 1 <= last:
+                jobs(k + 1)
+            if k in quant_v:
+                quantize_v(1, quant_v[k])
+            if k >= 5 and phase in (1, 2):
+                quantize_y((2 * b + phase - 1) % RING, 4 * b + 2 * (phase - 1), 2)
+            if k == last:
+                total_bf16(k)
+            total(k)
+            if k < last:
+                cast(k)
+            if k in gpsimd_v:
+                g, a = gpsimd_v[k]
+                interleave_v("gpsimd", 1, g, a, a + 128)
+            store_y(k)
+            if k >= 5 and phase == 2:
+                store_words(4 * b, 4)
+                if 4 * b + 4 == TILES:
+                    store_scales(0, [nc.sync] * 4)
+            if k >= 5 and phase == 0:
+                gather((2 * b) % RING, turn_banks[0], 2)
+            if k + 2 <= last:
+                square(k + 2)
+            if k in scalar_v:
+                g, a = scalar_v[k]
+                interleave_v("scalar", 1, g, a, a + 128)
+            if k >= 5 and phase == 0:
+                gather((2 * b + 1) % RING, turn_banks[1], 2)
+            if k + 2 <= last:
+                invert(k + 2)
+
+        turn(turn_banks[0], last - 3, 2)
+        turn(turn_banks[1], last - 1, 1)
+        turn(rho_banks[0], last, 1)
+        gather(2, turn_banks[0], 2)
+        gather(3, turn_banks[1], 1)
+        gather(0, rho_banks[0], 1)
+        quantize_y(2, last - 3, 2)
+        quantize_y(3, last - 1, 1)
+        store_words(last - 3, 3)
+        quantize_y(0, last, 1)
+        store_words(last, 1)
+        store_scales(1, [nc.sync, nc.scalar, nc.sync, nc.scalar])

@@ -21,7 +21,7 @@ PASSES = 2
 HALF = 512
 TILES = T // P
 UNITS = 2 * TILES
-X_CHUNKS = ((0, 384), (384, 896), (896, 1536))
+X_CHUNKS = ((0, 256), (256, 512), (512, 1024), (1024, 1536))
 RING = 4
 YB_RING = 8
 
@@ -60,7 +60,7 @@ def tile_jackson_congestion_cost_k3_kernel(
         cost_t = [sb("cost%d" % j, [P, HALF], F32) for j in range(RING)]
         y_t = [sb("y%d" % j, [P, HALF], F32) for j in range(UNITS)]
         yb_t = [sb("yb%d" % j, [P, HALF], BF16) for j in range(YB_RING)]
-        y_grp = [sb("ygrp%d" % j, [P, 2 * HALF], BF16) for j in range(RING)]
+        y_grp = [sb("ygrp%d" % j, [P, 4 * HALF], BF16) for j in range(2)]
         yw = [sb("yw%d" % h, [P, T], U32) for h in range(2)]
         ys = [sb("ys%d" % h, [P, T], U8) for h in range(2)]
 
@@ -166,8 +166,11 @@ def tile_jackson_congestion_cost_k3_kernel(
         def pairs_out(u):
             return yb_t[u % YB_RING][:].rearrange("p (w m e) -> p w m e", w=2, e=2)
 
-        def cast(u):
-            nc.gpsimd.tensor_scalar(pairs_out(u), pairs_in(y_t[u][:]), 1.0, 1.0, ALU.mult, ALU.mult)
+        def cast(u, engine="gpsimd"):
+            if engine == "gpsimd":
+                nc.gpsimd.tensor_scalar(pairs_out(u), pairs_in(y_t[u][:]), 1.0, 1.0, ALU.mult, ALU.mult)
+            else:
+                nc.scalar.copy(out=pairs_out(u), in_=pairs_in(y_t[u][:]))
 
         def total_bf16(u):
             nc.vector.tensor_tensor(
@@ -185,27 +188,31 @@ def tile_jackson_congestion_cost_k3_kernel(
                     c0 = (2 * i + w) * P
                     nc.tensor.transpose(bank[:, c0 : c0 + P], words[:, w * P : (w + 1) * P], ident[:])
 
-        def gather(slot, bank, n):
-            dst = y_grp[slot][:, 0 : n * HALF].bitcast(F32).rearrange("p (i m w) -> p i m w", i=n, w=2)
+        def grouped(u0, n):
+            return y_grp[(u0 // 4) % 2][:, (u0 % 4) * HALF : (u0 % 4 + n) * HALF]
+
+        def gather(bank, u0, n):
+            dst = grouped(u0, n).bitcast(F32).rearrange("p (i m w) -> p i m w", i=n, w=2)
             src = bank[:, 0 : n * 2 * P].rearrange("p (i w m) -> p i m w", i=n, w=2)
             nc.scalar.copy(out=dst, in_=src)
 
-        def quantize_y(slot, u0, n):
+        def quantize_y(u0, n):
             h, i = divmod(u0, TILES)
             cols = slice(i * P, (i + n) * P)
-            nc.vector.quantize_mx(
-                out=yw[h][:, cols].bitcast(FP8X4), scales=ys[h][:, cols], in_=y_grp[slot][:, 0 : n * HALF]
-            )
+            nc.vector.quantize_mx(out=yw[h][:, cols].bitcast(FP8X4), scales=ys[h][:, cols], in_=grouped(u0, n))
 
         def store_words(u0, n):
             h, i = divmod(u0, TILES)
             dst = out_1[h].rearrange("p m t -> p (m t)")[:, 4 * i * P : 4 * (i + n) * P]
             nc.sync.dma_start(out=dst.bitcast(I32), in_=yw[h][:, i * P : (i + n) * P].bitcast(I32))
 
-        def store_scales(h, queues):
+        def store_scales(u0, n, queues):
+            h, i = divmod(u0, TILES)
+            cols = slice(i * P, (i + n) * P)
             for q in range(4):
                 queues[q].dma_start(
-                    out=out_2[h, 4 * q : 4 * q + 4, :].bitcast(I32), in_=ys[h][32 * q : 32 * q + 4, :].bitcast(I32)
+                    out=out_2[h, 4 * q : 4 * q + 4, cols].bitcast(I32),
+                    in_=ys[h][32 * q : 32 * q + 4, cols].bitcast(I32),
                 )
 
         load_v(0, 0)
@@ -219,12 +226,13 @@ def tile_jackson_congestion_cost_k3_kernel(
         load_x(0)
         load_scales(cs, c_scales)
         load_c(0)
+        load_x(1)
         load_scales(es, e_scales)
         load_e(0)
-        load_x(1)
+        load_x(2)
         load_v(1, 0)
         load_v(1, 1)
-        load_x(2)
+        load_x(3)
         load_c(1)
         load_e(1)
 
@@ -234,73 +242,73 @@ def tile_jackson_congestion_cost_k3_kernel(
         interleave_v("scalar", 0, 1, 256, 512)
         interleave_v("vector", 0, 1, 0, 256)
         quantize_v(0, 1)
-        rho_pass(0, 0)
-        rho_pass(1, 0)
-        rho_pass(0, 1)
-        rho_pass(1, 1)
+        rho(0)
+        rho(1)
         square(0)
         invert(0)
         square(1)
         invert(1)
         jobs(0)
 
-        scalar_v = {2: (0, 256), 3: (0, 384), 4: (1, 128), 7: (1, 256), 8: (1, 384)}
-        gpsimd_v = {1: (0, 0), 2: (0, 128), 3: (1, 0)}
-        quant_v = {5: 0, 9: 1}
+        scalar_v = {2: (0, 256), 3: (0, 384), 4: (1, 128), 6: (1, 384)}
+        gpsimd_v = {1: (0, 0), 2: (0, 128), 3: (1, 0), 6: (1, 256)}
+        quant_v = {5: 0, 8: 1}
         last = UNITS - 1
-        for k in range(UNITS):
+        for k in range(last):
             b, phase = divmod(k - 5, 4)
             price(k)
-            if k == 0:
-                charge(0)
-            if k >= 5 and phase == 0:
-                turn(turn_banks[0], 4 * b, 2)
-                turn(turn_banks[1], 4 * b + 2, 2)
+            charge(k)
             if k + 2 <= last:
                 rho(k + 2)
-            if k > 0:
-                charge(k)
+            if b >= 0 and phase == 0:
+                turn(turn_banks[0], 4 * b, 2)
+                turn(turn_banks[1], 4 * b + 2, 2)
             cost(k)
-            if k + 1 <= last:
-                jobs(k + 1)
+            jobs(k + 1)
+            total(k)
+            store_y(k)
             if k in quant_v:
                 quantize_v(1, quant_v[k])
-            if k >= 5 and phase in (1, 2):
-                quantize_y((2 * b + phase - 1) % RING, 4 * b + 2 * (phase - 1), 2)
-            if k == last:
-                total_bf16(k)
-            total(k)
-            if k < last:
+            if b >= 0 and phase == 1 and k < last - 1:
+                quantize_y(4 * b, 4)
+                store_words(4 * b, 4)
+                if 4 * b + 4 == TILES:
+                    store_scales(0, TILES, [nc.sync] * 4)
+            if k < last - 1:
                 cast(k)
             if k in gpsimd_v:
                 g, a = gpsimd_v[k]
                 interleave_v("gpsimd", 1, g, a, a + 128)
-            store_y(k)
-            if k >= 5 and phase == 2:
-                store_words(4 * b, 4)
-                if 4 * b + 4 == TILES:
-                    store_scales(0, [nc.sync] * 4)
-            if k >= 5 and phase == 0:
-                gather((2 * b) % RING, turn_banks[0], 2)
             if k + 2 <= last:
                 square(k + 2)
+            if b >= 0 and phase == 0:
+                gather(turn_banks[0], 4 * b, 2)
             if k in scalar_v:
                 g, a = scalar_v[k]
                 interleave_v("scalar", 1, g, a, a + 128)
-            if k >= 5 and phase == 0:
-                gather((2 * b + 1) % RING, turn_banks[1], 2)
             if k + 2 <= last:
                 invert(k + 2)
+            if b >= 0 and phase == 0:
+                gather(turn_banks[1], 4 * b + 2, 2)
 
+        price(last)
+        charge(last)
         turn(turn_banks[0], last - 3, 2)
+        gather(turn_banks[0], last - 3, 2)
+        cast(last - 1, "scalar")
+        cost(last)
+        quantize_y(last - 7, 4)
+        store_words(last - 7, 4)
+        store_scales(TILES, 8, [nc.sync] * 4)
+        total_bf16(last)
+        total(last)
+        store_y(last)
         turn(turn_banks[1], last - 1, 1)
         turn(rho_banks[0], last, 1)
-        gather(2, turn_banks[0], 2)
-        gather(3, turn_banks[1], 1)
-        gather(0, rho_banks[0], 1)
-        quantize_y(2, last - 3, 2)
-        quantize_y(3, last - 1, 1)
-        store_words(last - 3, 3)
-        quantize_y(0, last, 1)
-        store_words(last, 1)
-        store_scales(1, [nc.sync, nc.scalar, nc.sync, nc.scalar])
+        gather(turn_banks[1], last - 1, 1)
+        gather(rho_banks[0], last, 1)
+        quantize_y(last - 3, 2)
+        store_words(last - 3, 2)
+        quantize_y(last - 1, 2)
+        store_words(last - 1, 2)
+        store_scales(last - 3, 4, [nc.scalar, nc.sync, nc.scalar, nc.scalar])

@@ -58,6 +58,7 @@ def tile_jackson_congestion_cost_k3_kernel(
         inv_t = [sb("inv%d" % j, [P, HALF], F32) for j in range(RING)]
         jobs_t = [sb("jobs%d" % j, [P, HALF], F32) for j in range(RING)]
         cost_t = [sb("cost%d" % j, [P, HALF], F32) for j in range(RING)]
+        charge_t = [sb("charge%d" % j, [P, HALF], F32) for j in range(2)]
         y_t = [sb("y%d" % j, [P, HALF], F32) for j in range(UNITS)]
         yb_t = [sb("yb%d" % j, [P, HALF], BF16) for j in range(YB_RING)]
         y_grp = [sb("ygrp%d" % j, [P, 4 * HALF], BF16) for j in range(2)]
@@ -160,6 +161,12 @@ def tile_jackson_congestion_cost_k3_kernel(
         def total(u):
             nc.vector.tensor_tensor(y_t[u][:], charge_banks[u % 2][:], cost_t[u % RING][:], ALU.add)
 
+        def keep_charge(u):
+            nc.scalar.copy(out=charge_t[u % 2][:], in_=charge_banks[u % 2][:])
+
+        def total_pool(u):
+            nc.gpsimd.tensor_tensor(y_t[u][:], charge_t[u % 2][:], cost_t[u % RING][:], ALU.add)
+
         def pairs_in(ap):
             return ap.rearrange("p (m w e) -> p w m e", w=2, e=2)
 
@@ -250,52 +257,64 @@ def tile_jackson_congestion_cost_k3_kernel(
         invert(1)
         jobs(0)
 
-        scalar_v = {2: (0, 256), 3: (0, 384), 4: (1, 128), 6: (1, 384)}
-        gpsimd_v = {1: (0, 0), 2: (0, 128), 3: (1, 0), 6: (1, 256)}
-        quant_v = {5: 0, 8: 1}
+        scalar_v = {2: (0, 128), 3: (0, 384), 4: (1, 0), 5: (1, 256)}
+        gpsimd_v = {1: (0, 0), 2: (0, 256), 4: (1, 128), 6: (1, 384)}
+        quant_v = {6: 0, 8: 1}
+        pool_add = (8, 12, 16, 20)
         last = UNITS - 1
         for k in range(last):
-            b, phase = divmod(k - 5, 4)
+            b, phase = divmod(k - 6, 4)
+            turning = b >= 0 and phase == 0
             price(k)
-            charge(k)
+            if turning:
+                charge(k)
             if k + 2 <= last:
                 rho(k + 2)
-            if b >= 0 and phase == 0:
+            if turning:
                 turn(turn_banks[0], 4 * b, 2)
                 turn(turn_banks[1], 4 * b + 2, 2)
-            cost(k)
-            jobs(k + 1)
-            total(k)
-            store_y(k)
+            else:
+                charge(k)
+            if k in pool_add:
+                jobs(k + 1)
+                cost(k)
+            else:
+                cost(k)
+                jobs(k + 1)
+                total(k)
+                store_y(k)
             if k in quant_v:
                 quantize_v(1, quant_v[k])
-            if b >= 0 and phase == 1 and k < last - 1:
+            if b >= 0 and phase == 1:
                 quantize_y(4 * b, 4)
                 store_words(4 * b, 4)
                 if 4 * b + 4 == TILES:
                     store_scales(0, TILES, [nc.sync] * 4)
-            if k < last - 1:
-                cast(k)
-            if k in gpsimd_v:
-                g, a = gpsimd_v[k]
-                interleave_v("gpsimd", 1, g, a, a + 128)
             if k + 2 <= last:
                 square(k + 2)
-            if b >= 0 and phase == 0:
+            if k in pool_add:
+                keep_charge(k)
+            if turning:
                 gather(turn_banks[0], 4 * b, 2)
             if k in scalar_v:
                 g, a = scalar_v[k]
                 interleave_v("scalar", 1, g, a, a + 128)
             if k + 2 <= last:
                 invert(k + 2)
-            if b >= 0 and phase == 0:
+            if turning:
                 gather(turn_banks[1], 4 * b + 2, 2)
+            if k in pool_add:
+                total_pool(k)
+                store_y(k)
+            cast(k, "scalar" if k == last - 1 else "gpsimd")
+            if k in gpsimd_v:
+                g, a = gpsimd_v[k]
+                interleave_v("gpsimd", 1, g, a, a + 128)
 
         price(last)
         charge(last)
         turn(turn_banks[0], last - 3, 2)
         gather(turn_banks[0], last - 3, 2)
-        cast(last - 1, "scalar")
         cost(last)
         quantize_y(last - 7, 4)
         store_words(last - 7, 4)

from contextlib import ExitStack

import concourse.mybir as mybir
from concourse.masks import make_identity

T, K = 1536, 1024
FLOPS = 3 * 2 * T * K * K

F32 = mybir.dt.float32
BF16 = mybir.dt.bfloat16
I32 = mybir.dt.int32
U32 = mybir.dt.uint32
U8 = mybir.dt.uint8
FP8X4 = mybir.dt.float8_e4m3fn_x4
FP4X4 = mybir.dt.float4_e2m1fn_x4
ALU = mybir.AluOpType
ACT = mybir.ActivationFunctionType

P = 128
PASSES = 2
HALF = 512
TILES = T // P
UNITS = 2 * TILES
X_CHUNKS = ((0, 256), (256, 512), (512, 1024), (1024, 1536))
RING = 4
YB_RING = 8


def tile_jackson_congestion_cost_k3_kernel(
    tc, x_words, x_scales, v, c_words, c_scales, e_words, e_scales, out_0, out_1, out_2
):
    nc = tc.nc
    with ExitStack() as ctx:
        keep = ctx.enter_context(tc.tile_pool(name="keep", bufs=1))
        psum = ctx.enter_context(tc.psum_pool(name="psum", bufs=1))
        ctx.enter_context(tc.manual_schedule())

        def sb(name, shape, dtype):
            return keep.tile(shape, dtype, name=name, align_bytes=64)

        banks = [psum.tile([P, HALF], F32, name="bank%d" % b) for b in range(8)]
        rho_banks, price_banks, charge_banks, turn_banks = banks[0:2], banks[2:4], banks[4:6], banks[6:8]

        xw = [sb("xw%d" % j, [P, PASSES, b - a], U32) for j, (a, b) in enumerate(X_CHUNKS)]
        xs = sb("xs", [P, PASSES, T], U8)
        cw = [sb("cw%d" % h, [P, PASSES, 2 * HALF], U8) for h in range(2)]
        cs = sb("cs", [P, PASSES, K], U8)
        ew = [sb("ew%d" % h, [P, PASSES, HALF], U32) for h in range(2)]
        es = sb("es", [P, PASSES, K], U8)
        v_raw = [[sb("vraw%d%d" % (h, g), [P, 4, HALF], BF16) for g in range(PASSES)] for h in range(2)]
        v_grp = [[sb("vgrp%d%d" % (h, g), [P, HALF, 4], BF16) for g in range(PASSES)] for h in range(2)]
        vw = [[sb("vw%d%d" % (h, g), [P, HALF], U32) for g in range(PASSES)] for h in range(2)]
        vs = [[sb("vs%d%d" % (h, g), [P, HALF], U8) for g in range(PASSES)] for h in range(2)]
        one = sb("one", [P, 1], F32)
        warm = sb("warm", [P, 1], F32)
        ident = sb("ident", [P, P], F32)
        sq_t = [sb("sq%d" % j, [P, HALF], F32) for j in range(RING)]
        inv_t = [sb("inv%d" % j, [P, HALF], F32) for j in range(RING)]
        jobs_t = [sb("jobs%d" % j, [P, HALF], F32) for j in range(RING)]
        cost_t = [sb("cost%d" % j, [P, HALF], F32) for j in range(RING)]
        charge_t = [sb("charge%d" % j, [P, HALF], F32) for j in range(2)]
        y_t = [sb("y%d" % j, [P, HALF], F32) for j in range(UNITS)]
        yb_t = [sb("yb%d" % j, [P, HALF], BF16) for j in range(YB_RING)]
        y_grp = [sb("ygrp%d" % j, [P, 4 * HALF], BF16) for j in range(2)]
        yw = [sb("yw%d" % h, [P, T], U32) for h in range(2)]
        ys = [sb("ys%d" % h, [P, T], U8) for h in range(2)]

        def load_v(h, g):
            rows = v[g * 512 : (g + 1) * 512, h * HALF : (h + 1) * HALF]
            nc.sync.dma_start(out=v_raw[h][g][:], in_=rows.rearrange("(p t) n -> p t n", t=4))

        def load_scales(plane, src):
            rows = src.rearrange("g (q r) n -> r q g n", r=4)
            for r in range(4):
                nc.sync.dma_start(out=plane[r:P:32, :, :].bitcast(I32), in_=rows[r].bitcast(I32))

        def load_x(j):
            a, b = X_CHUNKS[j]
            src = x_words.rearrange("g p n t -> p g (n t)")[:, :, 4 * a : 4 * b]
            nc.sync.dma_start(out=xw[j][:].bitcast(I32), in_=src.bitcast(I32))

        def load_c(h):
            src = c_words.rearrange("g p b -> p g b")[:, :, 2 * HALF * h : 2 * HALF * (h + 1)]
            nc.sync.dma_start(out=cw[h][:].bitcast(I32), in_=src.bitcast(I32))

        def load_e(h):
            src = e_words.rearrange("g p n t -> p g (n t)")[:, :, 4 * HALF * h : 4 * HALF * (h + 1)]
            nc.sync.dma_start(out=ew[h][:].bitcast(I32), in_=src.bitcast(I32))

        def interleave_v(engine, h, g, a, b):
            dst = v_grp[h][g][:, a:b, :]
            src = v_raw[h][g][:, :, a:b]
            if engine == "gpsimd":
                nc.gpsimd.tensor_scalar(dst, src.rearrange("p t n -> p n t"), 1.0, 1.0, ALU.mult, ALU.mult)
                return
            dst = dst.rearrange("p (c i) t -> p c t i", i=4)
            src = src.rearrange("p t (c i) -> p c t i", i=4)
            if engine == "vector":
                nc.vector.tensor_copy(out=dst, in_=src)
            else:
                nc.scalar.copy(out=dst, in_=src)

        def quantize_v(h, g):
            nc.vector.quantize_mx(
                out=vw[h][g][:].bitcast(FP8X4),
                scales=vs[h][g][:],
                in_=v_grp[h][g][:].rearrange("p n t -> p (n t)"),
            )

        def mx_pass(bank, u, g, rhs, rhs_scale):
            m0 = (u % TILES) * P
            j = [a <= m0 < b for a, b in X_CHUNKS].index(True)
            off = m0 - X_CHUNKS[j][0]
            nc.tensor.matmul_mx(
                out=bank[:],
                lhsT=xw[j][:, g, off : off + P].bitcast(FP8X4),
                lhsT_scale=xs[:, g, m0 : m0 + P],
                rhs=rhs,
                rhs_scale=rhs_scale,
                start=(g == 0),
                stop=(g == PASSES - 1),
            )

        def rho_bank(u):
            if u < 2:
                return rho_banks[u]
            if u == 2:
                return turn_banks[0]
            return rho_banks[(u + 1) % 2]

        def rho_pass(u, g):
            h = u // TILES
            mx_pass(rho_bank(u), u, g, vw[h][g][:].bitcast(FP8X4), vs[h][g][:])

        def rho(u):
            for g in range(PASSES):
                rho_pass(u, g)

        def price(u):
            h = u // TILES
            for g in range(PASSES):
                mx_pass(price_banks[u % 2], u, g, cw[h][:, g, :].bitcast(FP4X4), cs[:, g, h * HALF : (h + 1) * HALF])

        def charge(u):
            h = u // TILES
            for g in range(PASSES):
                mx_pass(charge_banks[u % 2], u, g, ew[h][:, g, :].bitcast(FP8X4), es[:, g, h * HALF : (h + 1) * HALF])

        def square(u):
            nc.scalar.activation(sq_t[u % RING][:], rho_bank(u)[:], ACT.Square, bias=one[:], scale=-1.0)

        def invert(u):
            nc.scalar.activation(inv_t[u % RING][:], sq_t[u % RING][:], ACT.Abs_reciprocal_sqrt)

        def jobs(u):
            nc.vector.tensor_tensor(jobs_t[u % RING][:], rho_bank(u)[:], inv_t[u % RING][:], ALU.mult)

        def cost(u):
            nc.vector.tensor_tensor(cost_t[u % RING][:], price_banks[u % 2][:], jobs_t[u % RING][:], ALU.mult)

        def total(u):
            nc.vector.tensor_tensor(y_t[u][:], charge_banks[u % 2][:], cost_t[u % RING][:], ALU.add)

        def keep_charge(u):
            nc.scalar.copy(out=charge_t[u % 2][:], in_=charge_banks[u % 2][:])

        def total_pool(u):
            nc.gpsimd.tensor_tensor(y_t[u][:], charge_t[u % 2][:], cost_t[u % RING][:], ALU.add)

        def pairs_in(ap):
            return ap.rearrange("p (m w e) -> p w m e", w=2, e=2)

        def pairs_out(u):
            return yb_t[u % YB_RING][:].rearrange("p (w m e) -> p w m e", w=2, e=2)

        def cast(u, engine="gpsimd"):
            if engine == "gpsimd":
                nc.gpsimd.tensor_scalar(pairs_out(u), pairs_in(y_t[u][:]), 1.0, 1.0, ALU.mult, ALU.mult)
            else:
                nc.scalar.copy(out=pairs_out(u), in_=pairs_in(y_t[u][:]))

        def total_bf16(u):
            nc.vector.tensor_tensor(
                pairs_out(u), pairs_in(charge_banks[u % 2][:]), pairs_in(cost_t[u % RING][:]), ALU.add
            )

        def store_y(u):
            h, i = divmod(u, TILES)
            nc.sync.dma_start(out=out_0[i * P : (i + 1) * P, h * HALF : (h + 1) * HALF], in_=y_t[u][:])

        def turn(bank, u0, n):
            for i in range(n):
                words = yb_t[(u0 + i) % YB_RING][:].bitcast(F32)
                for w in range(2):
                    c0 = (2 * i + w) * P
                    nc.tensor.transpose(bank[:, c0 : c0 + P], words[:, w * P : (w + 1) * P], ident[:])

        def grouped(u0, n):
            return y_grp[(u0 // 4) % 2][:, (u0 % 4) * HALF : (u0 % 4 + n) * HALF]

        def gather(bank, u0, n):
            dst = grouped(u0, n).bitcast(F32).rearrange("p (i m w) -> p i m w", i=n, w=2)
            src = bank[:, 0 : n * 2 * P].rearrange("p (i w m) -> p i m w", i=n, w=2)
            nc.scalar.copy(out=dst, in_=src)

        def quantize_y(u0, n):
            h, i = divmod(u0, TILES)
            cols = slice(i * P, (i + n) * P)
            nc.vector.quantize_mx(out=yw[h][:, cols].bitcast(FP8X4), scales=ys[h][:, cols], in_=grouped(u0, n))

        def store_words(u0, n):
            h, i = divmod(u0, TILES)
            dst = out_1[h].rearrange("p m t -> p (m t)")[:, 4 * i * P : 4 * (i + n) * P]
            nc.sync.dma_start(out=dst.bitcast(I32), in_=yw[h][:, i * P : (i + n) * P].bitcast(I32))

        def store_scales(u0, n, queues):
            h, i = divmod(u0, TILES)
            cols = slice(i * P, (i + n) * P)
            for q in range(4):
                queues[q].dma_start(
                    out=out_2[h, 4 * q : 4 * q + 4, cols].bitcast(I32),
                    in_=ys[h][32 * q : 32 * q + 4, cols].bitcast(I32),
                )

        load_v(0, 0)
        load_v(0, 1)
        nc.gpsimd.memset(one[:], 1.0)
        nc.scalar.activation(warm[:], one[:], ACT.Abs_reciprocal_sqrt)
        for plane in (xs, cs, es):
            nc.vector.memset(plane[:].bitcast(I32), 0)
        make_identity(nc, ident[:])
        load_scales(xs, x_scales)
        load_x(0)
        load_scales(cs, c_scales)
        load_c(0)
        load_x(1)
        load_scales(es, e_scales)
        load_e(0)
        load_x(2)
        load_v(1, 0)
        load_v(1, 1)
        load_x(3)
        load_c(1)
        load_e(1)

        interleave_v("vector", 0, 0, 0, 320)
        interleave_v("scalar", 0, 0, 320, 512)
        quantize_v(0, 0)
        interleave_v("scalar", 0, 1, 256, 512)
        interleave_v("vector", 0, 1, 0, 256)
        quantize_v(0, 1)
        rho(0)
        rho(1)
        square(0)
        invert(0)
        square(1)
        invert(1)
        jobs(0)

        scalar_v = {2: (0, 128), 3: (0, 384), 4: (1, 0), 5: (1, 256)}
        gpsimd_v = {1: (0, 0), 2: (0, 256), 4: (1, 128), 6: (1, 384)}
        quant_v = {6: 0, 8: 1}
        pool_add = (8, 12, 16, 20)
        last = UNITS - 1
        for k in range(last):
            b, phase = divmod(k - 6, 4)
            turning = b >= 0 and phase == 0
            price(k)
            if turning:
                charge(k)
            if k + 2 <= last:
                rho(k + 2)
            if turning:
                turn(turn_banks[0], 4 * b, 2)
                turn(turn_banks[1], 4 * b + 2, 2)
            else:
                charge(k)
            if k in pool_add:
                jobs(k + 1)
                cost(k)
            else:
                cost(k)
                jobs(k + 1)
                total(k)
                store_y(k)
            if k in quant_v:
                quantize_v(1, quant_v[k])
            if b >= 0 and phase == 1:
                quantize_y(4 * b, 4)
                store_words(4 * b, 4)
                if 4 * b + 4 == TILES:
                    store_scales(0, TILES, [nc.sync] * 4)
            if k + 2 <= last:
                square(k + 2)
            if k in pool_add:
                keep_charge(k)
            if turning:
                gather(turn_banks[0], 4 * b, 2)
            if k in scalar_v:
                g, a = scalar_v[k]
                interleave_v("scalar", 1, g, a, a + 128)
            if k + 2 <= last:
                invert(k + 2)
            if turning:
                gather(turn_banks[1], 4 * b + 2, 2)
            if k in pool_add:
                total_pool(k)
                store_y(k)
            cast(k, "scalar" if k == last - 1 else "gpsimd")
            if k in gpsimd_v:
                g, a = gpsimd_v[k]
                interleave_v("gpsimd", 1, g, a, a + 128)

        price(last)
        charge(last)
        turn(turn_banks[0], last - 3, 2)
        gather(turn_banks[0], last - 3, 2)
        cost(last)
        quantize_y(last - 7, 4)
        store_words(last - 7, 4)
        store_scales(TILES, 8, [nc.sync] * 4)
        total_bf16(last)
        total(last)
        store_y(last)
        turn(turn_banks[1], last - 1, 1)
        turn(rho_banks[0], last, 1)
        gather(turn_banks[1], last - 1, 1)
        gather(rho_banks[0], last, 1)
        quantize_y(last - 3, 2)
        store_words(last - 3, 2)
        quantize_y(last - 1, 2)
        store_words(last - 1, 2)
        store_scales(last - 3, 4, [nc.scalar, nc.sync, nc.scalar, nc.scalar])
